import numpy as np
import ml_dtypes


def mxq(x, axis, fmt="e4m3"):
    dtype, down = {"e4m3": (ml_dtypes.float8_e4m3fn, 7), "e5m2": (ml_dtypes.float8_e5m2, 14)}[fmt]
    v = np.moveaxis(np.asarray(x, np.float32).astype(ml_dtypes.bfloat16).astype(np.float64), axis, -1)
    blocks = v.reshape(v.shape[:-1] + (-1, 32))
    amax = np.abs(blocks).max(-1, keepdims=True)
    byte = np.maximum(np.where(amax > 0, np.frexp(amax)[1] - 1 + 127, 0) - down, 1)
    scale = np.exp2(byte - 127.0)
    codes = (blocks / scale).astype(np.float32).astype(dtype).astype(np.float64)
    return np.moveaxis((codes * scale).reshape(v.shape), -1, axis)


WIDE = False


def mx_kscale(k):
    if not WIDE:
        return np.ones(k)
    levels = np.array([10, -10, 5, -5, 0])
    if k % 512:
        return np.exp2(np.random.permutation(np.resize(levels, k // 32))).repeat(32)
    a = np.empty((k // 512, 16))
    for p in range(k // 512):
        a[p, :8] = np.random.permutation(np.resize(levels, 8))
        for g in range(8):
            far = levels[np.abs(levels - a[p, g]) >= 10]
            a[p, g + 8] = far[np.random.randint(len(far))]
    return np.exp2(a.ravel()).repeat(32)


BF16 = ml_dtypes.bfloat16


def bf(x):
    return np.asarray(x, np.float32).astype(BF16)


def f64(x):
    return np.asarray(x).astype(np.float64)

def planes(Y):
    n, m = Y.shape
    b = f64(bf(Y)).reshape(n // 32, 32, m)
    amax = np.abs(b).max(1)
    byte = np.clip(np.where(amax > 0, np.frexp(amax)[1] - 1 + 127 - 7, 1), 1, 254)
    codes = (b * np.exp2(127.0 - byte)[:, None, :]).reshape(n, m).astype(np.float32).astype(ml_dtypes.float8_e4m3fn).view(np.uint8)
    words = codes.reshape(n // 512, 128, 4, m).transpose(0, 1, 3, 2)
    return np.ascontiguousarray(words), np.ascontiguousarray(byte.astype(np.uint8).reshape(n // 512, 16, m))


B, L, G = 512, 512, 1024


def grid_gradient(coeffs_q, dx_q, dy_q):
    return coeffs_q @ dx_q, coeffs_q @ dy_q


def setup_inputs():
    s, t = mx_kscale(L), mx_kscale(G)
    return {
        "psi": bf(np.random.standard_normal((B, L)) * s),
        "kappa": bf(np.random.uniform(-2.0, -0.1, L)),
        "dx": bf(np.random.standard_normal((L, G)) / np.sqrt(L) / s[:, None]),
        "dy": bf(np.random.standard_normal((L, G)) / np.sqrt(L) / s[:, None]),
        "beta": bf(0.5 * np.random.standard_normal(G)),
        "wq": bf((1.0 + 0.1 * np.random.standard_normal(G)) * t),
        "p": bf(np.random.standard_normal((G, L)) / np.sqrt(G) / t[:, None]),
    }


def core(psi, kappa, dx, dy, beta, wq, p):
    psi, kappa, beta, wq = f64(psi), f64(kappa), f64(beta), f64(wq)
    zc = psi * kappa[None, :]
    dx_q = mxq(f64(dx), 0, "e4m3")
    dy_q = mxq(f64(dy), 0, "e4m3")
    px, py = grid_gradient(mxq(psi, 1, "e4m3"), dx_q, dy_q)
    zx, zy = grid_gradient(mxq(zc, 1, "e4m3"), dx_q, dy_q)
    jac = px * (zy + beta[None, :]) - py * zx
    jw = jac * wq[None, :]
    return -(mxq(jw, 1, "e4m3") @ mxq(f64(p), 0, "e4m3"))


def reference(psi, kappa, dx, dy, beta, wq, p):
    R_out = core(psi, kappa, dx, dy, beta, wq, p)
    words, scales = planes(R_out.T)
    return R_out, words, scales

@@ -1,0 +1,325 @@
+from contextlib import ExitStack
+
+import concourse.mybir as mybir
+from concourse.masks import make_identity
+
+B, L, G = 512, 512, 1024
+FLOPS = 5 * 2 * B * L * G
+
+F32 = mybir.dt.float32
+BF16 = mybir.dt.bfloat16
+U32 = mybir.dt.uint32
+I32 = mybir.dt.int32
+U8 = mybir.dt.uint8
+FP8X4 = mybir.dt.float8_e4m3fn_x4
+ADD = mybir.AluOpType.add
+SUB = mybir.AluOpType.subtract
+MULT = mybir.AluOpType.mult
+COPY = mybir.ActivationFunctionType.Copy
+IDENTITY = mybir.ActivationFunctionType.Identity
+
+P = 128
+H = 256
+
+
+def tile_barotropicvorticitytransformtendency_x1_kernel(
+    tc, psi, kappa, dx, dy, beta, wq, p, out_0, out_1, out_2
+):
+    nc = tc.nc
+    with ExitStack() as ctx:
+        ctx.enter_context(tc.manual_schedule())
+        keep = ctx.enter_context(tc.tile_pool(name="keep", bufs=1))
+        stage = ctx.enter_context(tc.tile_pool(name="stage", bufs=4))
+        prod = ctx.enter_context(tc.tile_pool(name="prod", bufs=3))
+        ps_s = ctx.enter_context(tc.psum_pool(name="ps_s", bufs=3))
+        ps_v = ctx.enter_context(tc.psum_pool(name="ps_v", bufs=3))
+        ps_o = ctx.enter_context(tc.psum_pool(name="ps_o", bufs=2))
+
+        ident = keep.tile([P, P], F32, name="ident")
+        kap = keep.tile([P, 4], BF16, name="kap")
+        wq_b = keep.tile([P, 2, 4], BF16, name="wq_b")
+        wq_f = keep.tile([P, 2, 4], F32, name="wq_f")
+        beta_b = keep.tile([P, 2, 4], BF16, name="beta_b")
+        bw_f = keep.tile([P, 2, 4], F32, name="bw_f")
+        psi_sb = keep.tile([P, 4, L], BF16, name="psi_sb", align_bytes=64)
+        psi_g = keep.tile([P, B, 4], BF16, name="psi_g", align_bytes=64)
+        zc_g = keep.tile([P, B, 4], BF16, name="zc_g", align_bytes=64)
+        psi_q = keep.tile([P, B], U32, name="psi_q", align_bytes=64)
+        psi_s = keep.tile([P, B], U8, name="psi_s", align_bytes=64)
+        zc_q = keep.tile([P, B], U32, name="zc_q", align_bytes=64)
+        zc_s = keep.tile([P, B], U8, name="zc_s", align_bytes=64)
+
+        raw, grp, cod, sca = {}, {}, {}, {}
+        for w in ("dx", "dy", "p"):
+            for g in (0, 1):
+                raw[w, g] = keep.tile([P, 4, 512], BF16, name="raw_%s%d" % (w, g), align_bytes=64)
+                grp[w, g] = keep.tile([P, 4, P, 4], BF16, name="grp_%s%d" % (w, g), align_bytes=64)
+                cod[w, g] = keep.tile([P, 512], U32, name="cod_%s%d" % (w, g), align_bytes=64)
+                sca[w, g] = keep.tile([P, 512], U8, name="sca_%s%d" % (w, g), align_bytes=64)
+        jw_g, jw_q, jw_s = {}, {}, {}
+        for g in (0, 1):
+            jw_g[g] = keep.tile([P, B, 4], BF16, name="jw_g%d" % g, align_bytes=64)
+            jw_q[g] = keep.tile([P, B], U32, name="jw_q%d" % g, align_bytes=64)
+            jw_s[g] = keep.tile([P, B], U8, name="jw_s%d" % g, align_bytes=64)
+        m_sb = {}
+        for g in (0, 1):
+            m_sb[g] = keep.tile([P, 4, 2, B], F32, name="m_sb%d" % g)
+        y_g = keep.tile([P, B, 4], BF16, name="y_g", align_bytes=64)
+        y_q = keep.tile([P, B], U32, name="y_q", align_bytes=64)
+        y_s = keep.tile([P, B], U8, name="y_s", align_bytes=64)
+
+        def load(w, ap, g):
+            nc.sync.dma_start(out=raw[w, g][:], in_=ap.rearrange("(p j) m -> p j m", j=4))
+
+        psi_v = psi.rearrange("(p c) l -> p c l", c=4)
+        nc.scalar.dma_start(out=kap[:], in_=kappa.rearrange("(p t) -> p t", t=4))
+        nc.scalar.dma_start(out=wq_b[:], in_=wq.rearrange("(g p t) -> p g t", g=2, t=4))
+        nc.scalar.dma_start(out=beta_b[:], in_=beta.rearrange("(g p t) -> p g t", g=2, t=4))
+        load("dx", dx[:, 0:512], 0)
+        nc.sync.dma_start(out=psi_sb[:, 0:2, :], in_=psi_v[:, 0:2, :])
+        nc.sync.dma_start(out=psi_sb[:, 2:4, :], in_=psi_v[:, 2:4, :])
+        load("dy", dy[:, 0:512], 0)
+        load("dx", dx[:, 512:1024], 1)
+        load("dy", dy[:, 512:1024], 1)
+        load("p", p[0:512, :], 0)
+        load("p", p[512:1024, :], 1)
+
+        make_identity(nc, ident[:])
+
+        def inter(eng, w, g, t0, t1):
+            o = grp[w, g][:, t0:t1, :, :]
+            i = raw[w, g][:].rearrange("p j (m t) -> p t m j", t=4)[:, t0:t1, :, :]
+            if t1 - t0 == 1:
+                o = grp[w, g][:, t0, :, :]
+                i = raw[w, g][:].rearrange("p j (m t) -> p t m j", t=4)[:, t0, :, :]
+            if eng == "v":
+                nc.vector.tensor_copy(out=o, in_=i)
+            else:
+                nc.scalar.copy(out=o, in_=i)
+
+        def quant(w, g, t0, t1):
+            c = slice(t0 * P, t1 * P)
+            nc.vector.quantize_mx(
+                out=cod[w, g][:, c].bitcast(FP8X4),
+                scales=sca[w, g][:, c],
+                in_=grp[w, g][:, t0:t1, :, :].rearrange("p t m j -> p (t m j)"),
+            )
+
+        words = psi_sb[:].rearrange("p c l -> p (c l)").bitcast(F32)
+
+        def turn(k):
+            xt = ps_o.tile([P, 512], F32, name="o_bank")
+            for c in (0, 1):
+                for u in (0, 1):
+                    w0 = 256 * (2 * k + c)
+                    s0 = P * (2 * c + u)
+                    nc.tensor.transpose(xt[:, s0 : s0 + P], words[:, w0 + u : w0 + 256 : 2], ident[:])
+            return xt
+
+        psi_w = psi_g[:].rearrange("p b t -> p (b t)").bitcast(F32).rearrange("p (r k c u) -> p r k c u", k=2, c=2, u=2)
+
+        def turn_out(eng, k, xt):
+            o = psi_w[:, :, k, :, :]
+            i = xt[:].rearrange("p (c u r) -> p r c u", c=2, u=2)
+            if eng == "v":
+                nc.vector.tensor_copy(out=o, in_=i)
+            else:
+                nc.scalar.copy(out=o, in_=i)
+
+        def mm(out, a, asc, b, bsc, start=True, stop=True):
+            nc.tensor.matmul_mx(
+                out=out, lhsT=a.bitcast(FP8X4), lhsT_scale=asc, rhs=b.bitcast(FP8X4), rhs_scale=bsc,
+                start=start, stop=stop,
+            )
+
+        def unit(g, b0, n, ts):
+            k = len(ts)
+            b = slice(b0, b0 + n)
+            sb, vb = [], []
+            parts = []
+            if n == B:
+                for i in (0, 1):
+                    sb.append(ps_s.tile([P, B], F32, name="s_bank"))
+                parts_s = [(ts[0], i, sb[i][:]) for i in (0, 1)]
+            else:
+                bank = ps_s.tile([P, k, 2, n], F32, name="s_bank")
+                parts_s = [(t, i, bank[:, j, i, :]) for j, t in enumerate(ts) for i in (0, 1)]
+            for t, i, o in parts_s:
+                w = ("dx", "dy")[i]
+                c = slice(t * P, (t + 1) * P)
+                mm(o, cod[w, g][:, c], sca[w, g][:, c], zc_q[:, b], zc_s[:, b])
+            if n == B:
+                for i in (0, 1):
+                    vb.append(ps_v.tile([P, B], F32, name="v_bank"))
+                parts_v = [(ts[0], i, vb[i][:]) for i in (0, 1)]
+            else:
+                vbank = ps_v.tile([P, k, 2, n], F32, name="v_bank")
+                parts_v = [(t, i, vbank[:, j, i, :]) for j, t in enumerate(ts) for i in (0, 1)]
+            for t, i, o in parts_v:
+                w = ("dy", "dx")[i]
+                c = slice(t * P, (t + 1) * P)
+                mm(o, cod[w, g][:, c], sca[w, g][:, c], psi_q[:, b], psi_s[:, b])
+            s = stage.tile([P, k, 2, n], F32, name="s_sb")
+            for t, i, o in parts_s:
+                j = ts.index(t)
+                if i == 0:
+                    nc.scalar.activation(out=s[:, j, 0, :], in_=o, func=COPY, scale=wq_f[:, g, t : t + 1])
+                else:
+                    nc.scalar.activation(
+                        out=s[:, j, 1, :], in_=o, func=IDENTITY, scale=wq_f[:, g, t : t + 1], bias=bw_f[:, g, t : t + 1]
+                    )
+            m = m_sb[g]
+            if n == B:
+                for i in (0, 1):
+                    nc.vector.tensor_tensor(out=m[:, ts[0], i, :], in0=vb[i][:], in1=s[:, 0, i, :], op=MULT)
+            else:
+                nc.vector.tensor_tensor(out=m[:, ts[0] : ts[0] + k, :, b], in0=vbank[:], in1=s[:], op=MULT)
+
+        def subtract(g, b0, n):
+            b = slice(b0, b0 + n)
+            nc.vector.tensor_tensor(
+                out=jw_g[g][:, b, :].rearrange("p (c i) t -> p c t i", i=4),
+                in0=m_sb[g][:, :, 1, b].rearrange("p t (c i) -> p c t i", i=4),
+                in1=m_sb[g][:, :, 0, b].rearrange("p t (c i) -> p c t i", i=4),
+                op=SUB,
+            )
+
+        def quant_jw(g, b0, n):
+            b = slice(b0, b0 + n)
+            nc.vector.quantize_mx(
+                out=jw_q[g][:, b].bitcast(FP8X4),
+                scales=jw_s[g][:, b],
+                in_=jw_g[g][:, b, :].rearrange("p b t -> p (b t)"),
+            )
+
+        def planes_mm(c):
+            bank = ps_o.tile([P, 512], F32, name="o_bank")
+            b = slice(c * P, (c + 1) * P)
+            for t in range(4):
+                l = slice(t * P, (t + 1) * P)
+                for g in (0, 1):
+                    mm(bank[:, l], cod["p", g][:, l], sca["p", g][:, l], jw_q[g][:, b], jw_s[g][:, b],
+                       start=g == 0, stop=g == 1)
+            return bank
+
+        def rows_mm(c, pool, gs=(0, 1), bank=None):
+            if bank is None:
+                if pool == "s":
+                    bank = ps_s.tile([P, B], F32, name="s_bank")
+                elif pool == "v":
+                    bank = ps_v.tile([P, B], F32, name="v_bank")
+                else:
+                    bank = ps_o.tile([P, B], F32, name="o_bank")
+            b = slice(c * P, (c + 1) * P)
+            for g in gs:
+                mm(bank[:], jw_q[g][:, b], jw_s[g][:, b], cod["p", g][:], sca["p", g][:], start=g == 0, stop=g == 1)
+            return bank
+
+        def negate(eng, out, in_):
+            if eng == "v":
+                nc.vector.tensor_scalar(out=out, in0=in_, scalar1=-1.0, scalar2=None, op0=MULT)
+            else:
+                nc.scalar.activation(out=out, in_=in_, func=COPY, scale=-1.0)
+
+        def planes_out(eng, c, bank):
+            negate(eng, y_g[:, c * P : (c + 1) * P, :], bank[:].rearrange("p (t b) -> p b t", t=4))
+
+        def rows_out(eng, q, c, bank):
+            r = stage.tile([P, 512], F32, name="rows")
+            negate(eng, r[:].rearrange("p (m t) -> p m t", t=4), bank[:].rearrange("p (t m) -> p m t", t=4))
+            q.dma_start(out=out_0[c * P : (c + 1) * P, :], in_=r[:])
+
+        def quant_y(b0, n):
+            b = slice(b0, b0 + n)
+            nc.vector.quantize_mx(
+                out=y_q[:, b].bitcast(FP8X4), scales=y_s[:, b], in_=y_g[:, b, :].rearrange("p b t -> p (b t)")
+            )
+
+        def store_words(q, b0, n):
+            b = slice(b0, b0 + n)
+            q.dma_start(out=out_1[0, :, b, :].rearrange("p b t -> p (b t)").bitcast(I32), in_=y_q[:, b].bitcast(I32))
+
+        def store_scales(q, b0, n):
+            b = slice(b0, b0 + n)
+            for i in range(4):
+                q.dma_start(
+                    out=out_2[0, 4 * i : 4 * i + 4, b].bitcast(I32), in_=y_s[32 * i : 32 * i + 4, b].bitcast(I32)
+                )
+
+        def quant_all(q, s, g):
+            nc.vector.quantize_mx(out=q[:].bitcast(FP8X4), scales=s[:], in_=g[:].rearrange("p b t -> p (b t)"))
+
+        nc.scalar.activation(out=wq_f[:], in_=wq_b[:], func=COPY)
+        nc.gpsimd.tensor_tensor(out=bw_f[:], in0=beta_b[:], in1=wq_b[:], op=MULT)
+        inter("v", "dx", 0, 0, 2)
+        inter("s", "dx", 0, 2, 4)
+        xt0 = turn(0)
+        xt1 = turn(1)
+        turn_out("v", 0, xt0)
+        turn_out("s", 1, xt1)
+        quant("dx", 0, 0, 4)
+        nc.vector.tensor_tensor(out=zc_g[:], in0=psi_g[:], in1=kap[:].unsqueeze(1).to_broadcast([P, B, 4]), op=MULT)
+        inter("s", "dy", 0, 2, 4)
+        inter("v", "dy", 0, 0, 2)
+        quant_all(zc_q, zc_s, zc_g)
+        quant("dy", 0, 0, 2)
+        quant_all(psi_q, psi_s, psi_g)
+        quant("dy", 0, 2, 4)
+        inter("s", "dx", 1, 0, 2)
+        unit(0, 0, B, [0])
+        inter("s", "dx", 1, 2, 3)
+        inter("v", "dx", 1, 3, 4)
+        unit(0, 0, B, [1])
+        quant("dx", 1, 0, 4)
+        inter("s", "dy", 1, 0, 2)
+        unit(0, 0, B, [2])
+        inter("v", "dy", 1, 3, 4)
+        inter("s", "dy", 1, 2, 3)
+        unit(0, 0, B, [3])
+        quant("dy", 1, 0, 4)
+        subtract(0, 0, 256)
+        inter("s", "p", 0, 0, 2)
+        inter("s", "p", 0, 2, 3)
+        unit(1, 0, 256, [0])
+        subtract(0, 256, 256)
+        unit(1, 0, 256, [1])
+        inter("s", "p", 1, 0, 2)
+        inter("v", "p", 0, 3, 4)
+        quant_jw(0, 0, 512)
+        unit(1, 0, 256, [2])
+        inter("s", "p", 1, 2, 4)
+        quant("p", 0, 0, 4)
+        unit(1, 0, 256, [3])
+        unit(1, 256, 128, [0, 1])
+        subtract(1, 0, 256)
+        unit(1, 256, 128, [2, 3])
+        quant_jw(1, 0, 256)
+        quant("p", 1, 0, 4)
+        unit(1, 384, 128, [0, 1])
+        subtract(1, 256, 128)
+        unit(1, 384, 128, [2, 3])
+        quant_jw(1, 256, 128)
+        k0 = planes_mm(0)
+        planes_out("s", 0, k0)
+        k1 = planes_mm(1)
+        planes_out("s", 1, k1)
+        subtract(1, 384, 128)
+        r0 = rows_mm(0, "s")
+        rows_out("s", nc.sync, 0, r0)
+        r1 = rows_mm(1, "s")
+        rows_out("v", nc.sync, 1, r1)
+        quant_jw(1, 384, 128)
+        k2 = planes_mm(2)
+        planes_out("s", 2, k2)
+        quant_y(0, 256)
+        store_words(nc.sync, 0, 256)
+        store_scales(nc.sync, 0, 256)
+        r2 = rows_mm(2, "v")
+        k3 = planes_mm(3)
+        r3 = rows_mm(3, "s")
+        rows_out("v", nc.sync, 2, r2)
+        planes_out("s", 3, k3)
+        rows_out("v", nc.sync, 3, r3)
+        quant_y(256, 256)
+        store_words(nc.sync, 256, 256)
+        store_scales(nc.scalar, 256, 256)

@@ -86,12 +86,9 @@ def tile_barotropicvorticitytransformtendency_x1_kernel(
 
         make_identity(nc, ident[:])
 
-        def inter(eng, w, g, t0, t1):
-            o = grp[w, g][:, t0:t1, :, :]
-            i = raw[w, g][:].rearrange("p j (m t) -> p t m j", t=4)[:, t0:t1, :, :]
-            if t1 - t0 == 1:
-                o = grp[w, g][:, t0, :, :]
-                i = raw[w, g][:].rearrange("p j (m t) -> p t m j", t=4)[:, t0, :, :]
+        def inter(eng, w, g, m0, m1):
+            o = grp[w, g][:].rearrange("p t m j -> p m t j")[:, m0:m1]
+            i = raw[w, g][:].rearrange("p j (m t) -> p m t j", t=4)[:, m0:m1]
             if eng == "v":
                 nc.vector.tensor_copy(out=o, in_=i)
             else:
@@ -251,43 +248,41 @@ def tile_barotropicvorticitytransformtendency_x1_kernel(
 
         nc.scalar.activation(out=wq_f[:], in_=wq_b[:], func=COPY)
         nc.gpsimd.tensor_tensor(out=bw_f[:], in0=beta_b[:], in1=wq_b[:], op=MULT)
-        inter("v", "dx", 0, 0, 2)
-        inter("s", "dx", 0, 2, 4)
+        inter("v", "dx", 0, 0, 64)
+        inter("s", "dx", 0, 64, 128)
         xt0 = turn(0)
         xt1 = turn(1)
         turn_out("v", 0, xt0)
         turn_out("s", 1, xt1)
         quant("dx", 0, 0, 4)
         nc.vector.tensor_tensor(out=zc_g[:], in0=psi_g[:], in1=kap[:].unsqueeze(1).to_broadcast([P, B, 4]), op=MULT)
-        inter("s", "dy", 0, 2, 4)
-        inter("v", "dy", 0, 0, 2)
+        inter("s", "dy", 0, 64, 128)
+        inter("v", "dy", 0, 0, 64)
         quant_all(zc_q, zc_s, zc_g)
-        quant("dy", 0, 0, 2)
+        quant("dy", 0, 0, 4)
         quant_all(psi_q, psi_s, psi_g)
-        quant("dy", 0, 2, 4)
-        inter("s", "dx", 1, 0, 2)
+        inter("s", "dx", 1, 32, 96)
         unit(0, 0, B, [0])
-        inter("s", "dx", 1, 2, 3)
-        inter("v", "dx", 1, 3, 4)
+        inter("s", "dx", 1, 96, 128)
+        inter("v", "dx", 1, 0, 32)
         unit(0, 0, B, [1])
         quant("dx", 1, 0, 4)
-        inter("s", "dy", 1, 0, 2)
+        inter("s", "dy", 1, 32, 96)
         unit(0, 0, B, [2])
-        inter("v", "dy", 1, 3, 4)
-        inter("s", "dy", 1, 2, 3)
+        inter("v", "dy", 1, 0, 32)
+        inter("s", "dy", 1, 96, 128)
         unit(0, 0, B, [3])
         quant("dy", 1, 0, 4)
         subtract(0, 0, 256)
-        inter("s", "p", 0, 0, 2)
-        inter("s", "p", 0, 2, 3)
+        inter("s", "p", 0, 32, 128)
         unit(1, 0, 256, [0])
         subtract(0, 256, 256)
         unit(1, 0, 256, [1])
-        inter("s", "p", 1, 0, 2)
-        inter("v", "p", 0, 3, 4)
+        inter("s", "p", 1, 0, 64)
+        inter("v", "p", 0, 0, 32)
         quant_jw(0, 0, 512)
         unit(1, 0, 256, [2])
-        inter("s", "p", 1, 2, 4)
+        inter("s", "p", 1, 64, 128)
         quant("p", 0, 0, 4)
         unit(1, 0, 256, [3])
         unit(1, 256, 128, [0, 1])

@@ -86,13 +86,12 @@ def tile_barotropicvorticitytransformtendency_x1_kernel(
 
         make_identity(nc, ident[:])
 
-        def inter(eng, w, g, m0, m1):
-            o = grp[w, g][:].rearrange("p t m j -> p m t j")[:, m0:m1]
-            i = raw[w, g][:].rearrange("p j (m t) -> p m t j", t=4)[:, m0:m1]
-            if eng == "v":
-                nc.vector.tensor_copy(out=o, in_=i)
-            else:
-                nc.scalar.copy(out=o, in_=i)
+        def inter(w, g, cut):
+            o = grp[w, g][:].rearrange("p t m j -> p m t j")
+            i = raw[w, g][:].rearrange("p j (m t) -> p m t j", t=4)
+            if cut > 0:
+                nc.vector.tensor_copy(out=o[:, 0:cut], in_=i[:, 0:cut])
+            nc.scalar.copy(out=o[:, cut:P], in_=i[:, cut:P])
 
         def quant(w, g, t0, t1):
             c = slice(t0 * P, t1 * P)
@@ -172,9 +171,9 @@ def tile_barotropicvorticitytransformtendency_x1_kernel(
             else:
                 nc.vector.tensor_tensor(out=m[:, ts[0] : ts[0] + k, :, b], in0=vbank[:], in1=s[:], op=MULT)
 
-        def subtract(g, b0, n):
+        def subtract(eng, g, b0, n):
             b = slice(b0, b0 + n)
-            nc.vector.tensor_tensor(
+            eng.tensor_tensor(
                 out=jw_g[g][:, b, :].rearrange("p (c i) t -> p c t i", i=4),
                 in0=m_sb[g][:, :, 1, b].rearrange("p t (c i) -> p c t i", i=4),
                 in1=m_sb[g][:, :, 0, b].rearrange("p t (c i) -> p c t i", i=4),
@@ -221,10 +220,10 @@ def tile_barotropicvorticitytransformtendency_x1_kernel(
         def planes_out(eng, c, bank):
             negate(eng, y_g[:, c * P : (c + 1) * P, :], bank[:].rearrange("p (t b) -> p b t", t=4))
 
-        def rows_out(eng, q, c, bank):
-            r = stage.tile([P, 512], F32, name="rows")
-            negate(eng, r[:].rearrange("p (m t) -> p m t", t=4), bank[:].rearrange("p (t m) -> p m t", t=4))
-            q.dma_start(out=out_0[c * P : (c + 1) * P, :], in_=r[:])
+        def rows_out(eng, c, bank):
+            rows = stage.tile([P, 512], F32, name="rows")
+            negate(eng, rows[:].rearrange("p (m t) -> p m t", t=4), bank[:].rearrange("p (t m) -> p m t", t=4))
+            nc.sync.dma_start(out=out_0[c * P : (c + 1) * P, :], in_=rows[:])
 
         def quant_y(b0, n):
             b = slice(b0, b0 + n)
@@ -248,73 +247,65 @@ def tile_barotropicvorticitytransformtendency_x1_kernel(
 
         nc.scalar.activation(out=wq_f[:], in_=wq_b[:], func=COPY)
         nc.gpsimd.tensor_tensor(out=bw_f[:], in0=beta_b[:], in1=wq_b[:], op=MULT)
-        inter("v", "dx", 0, 0, 64)
-        inter("s", "dx", 0, 64, 128)
+        inter("dx", 0, 64)
         xt0 = turn(0)
         xt1 = turn(1)
-        turn_out("v", 0, xt0)
-        turn_out("s", 1, xt1)
         quant("dx", 0, 0, 4)
-        nc.vector.tensor_tensor(out=zc_g[:], in0=psi_g[:], in1=kap[:].unsqueeze(1).to_broadcast([P, B, 4]), op=MULT)
-        inter("s", "dy", 0, 64, 128)
-        inter("v", "dy", 0, 0, 64)
-        quant_all(zc_q, zc_s, zc_g)
-        quant("dy", 0, 0, 4)
+        turn_out("s", 0, xt0)
+        turn_out("v", 1, xt1)
+        inter("dy", 0, 72)
         quant_all(psi_q, psi_s, psi_g)
-        inter("s", "dx", 1, 32, 96)
-        unit(0, 0, B, [0])
-        inter("s", "dx", 1, 96, 128)
-        inter("v", "dx", 1, 0, 32)
-        unit(0, 0, B, [1])
+        nc.vector.tensor_tensor(out=zc_g[:], in0=psi_g[:], in1=kap[:].unsqueeze(1).to_broadcast([P, B, 4]), op=MULT)
+        quant("dy", 0, 0, 4)
+        inter("dx", 1, 48)
+        quant_all(zc_q, zc_s, zc_g)
+        inter("dy", 1, 80)
         quant("dx", 1, 0, 4)
-        inter("s", "dy", 1, 32, 96)
-        unit(0, 0, B, [2])
-        inter("v", "dy", 1, 0, 32)
-        inter("s", "dy", 1, 96, 128)
-        unit(0, 0, B, [3])
+        inter("p", 0, 64)
+        unit(0, 0, B, [0])
+        unit(0, 0, B, [1])
         quant("dy", 1, 0, 4)
-        subtract(0, 0, 256)
-        inter("s", "p", 0, 32, 128)
-        unit(1, 0, 256, [0])
-        subtract(0, 256, 256)
-        unit(1, 0, 256, [1])
-        inter("s", "p", 1, 0, 64)
-        inter("v", "p", 0, 0, 32)
-        quant_jw(0, 0, 512)
-        unit(1, 0, 256, [2])
-        inter("s", "p", 1, 64, 128)
+        unit(0, 0, B, [2])
+        unit(0, 0, B, [3])
+        for i in range(8):
+            subtract(nc.gpsimd, 0, 64 * i, 64)
         quant("p", 0, 0, 4)
+        inter("p", 1, 40)
+        unit(1, 0, 256, [0])
+        unit(1, 0, 256, [1])
+        unit(1, 0, 256, [2])
         unit(1, 0, 256, [3])
-        unit(1, 256, 128, [0, 1])
-        subtract(1, 0, 256)
-        unit(1, 256, 128, [2, 3])
-        quant_jw(1, 0, 256)
         quant("p", 1, 0, 4)
+        unit(1, 256, 128, [0, 1])
+        subtract(nc.vector, 1, 0, 256)
+        unit(1, 256, 128, [2, 3])
+        quant_jw(0, 0, 512)
+        quant_jw(1, 0, 256)
         unit(1, 384, 128, [0, 1])
-        subtract(1, 256, 128)
+        subtract(nc.vector, 1, 256, 128)
         unit(1, 384, 128, [2, 3])
-        quant_jw(1, 256, 128)
         k0 = planes_mm(0)
         planes_out("s", 0, k0)
+        r0 = rows_mm(0, "s")
+        rows_out("s", 0, r0)
+        quant_jw(1, 256, 128)
         k1 = planes_mm(1)
         planes_out("s", 1, k1)
-        subtract(1, 384, 128)
-        r0 = rows_mm(0, "s")
-        rows_out("s", nc.sync, 0, r0)
         r1 = rows_mm(1, "s")
-        rows_out("v", nc.sync, 1, r1)
-        quant_jw(1, 384, 128)
+        rows_out("s", 1, r1)
+        subtract(nc.vector, 1, 384, 128)
         k2 = planes_mm(2)
         planes_out("s", 2, k2)
+        quant_jw(1, 384, 128)
+        r2 = rows_mm(2, "v")
+        rows_out("s", 2, r2)
         quant_y(0, 256)
         store_words(nc.sync, 0, 256)
-        store_scales(nc.sync, 0, 256)
-        r2 = rows_mm(2, "v")
         k3 = planes_mm(3)
         r3 = rows_mm(3, "s")
-        rows_out("v", nc.sync, 2, r2)
-        planes_out("s", 3, k3)
-        rows_out("v", nc.sync, 3, r3)
-        quant_y(256, 256)
+        quant_y(256, 128)
+        planes_out("v", 3, k3)
+        rows_out("s", 3, r3)
+        quant_y(384, 128)
         store_words(nc.sync, 256, 256)
-        store_scales(nc.scalar, 256, 256)
+        store_scales(nc.sync, 0, 512)

@@ -72,26 +72,18 @@ def tile_barotropicvorticitytransformtendency_x1_kernel(
             nc.sync.dma_start(out=raw[w, g][:], in_=ap.rearrange("(p j) m -> p j m", j=4))
 
         psi_v = psi.rearrange("(p c) l -> p c l", c=4)
-        nc.scalar.dma_start(out=kap[:], in_=kappa.rearrange("(p t) -> p t", t=4))
-        nc.scalar.dma_start(out=wq_b[:], in_=wq.rearrange("(g p t) -> p g t", g=2, t=4))
-        nc.scalar.dma_start(out=beta_b[:], in_=beta.rearrange("(g p t) -> p g t", g=2, t=4))
-        load("dx", dx[:, 0:512], 0)
-        nc.sync.dma_start(out=psi_sb[:, 0:2, :], in_=psi_v[:, 0:2, :])
-        nc.sync.dma_start(out=psi_sb[:, 2:4, :], in_=psi_v[:, 2:4, :])
-        load("dy", dy[:, 0:512], 0)
-        load("dx", dx[:, 512:1024], 1)
-        load("dy", dy[:, 512:1024], 1)
-        load("p", p[0:512, :], 0)
-        load("p", p[512:1024, :], 1)
 
         make_identity(nc, ident[:])
 
-        def inter(w, g, cut):
-            o = grp[w, g][:].rearrange("p t m j -> p m t j")
-            i = raw[w, g][:].rearrange("p j (m t) -> p m t j", t=4)
-            if cut > 0:
-                nc.vector.tensor_copy(out=o[:, 0:cut], in_=i[:, 0:cut])
-            nc.scalar.copy(out=o[:, cut:P], in_=i[:, cut:P])
+        def inter(eng, w, g, m0, m1):
+            if m0 == m1:
+                return
+            o = grp[w, g][:].rearrange("p t m j -> p m t j")[:, m0:m1]
+            i = raw[w, g][:].rearrange("p j (m t) -> p m t j", t=4)[:, m0:m1]
+            if eng == "v":
+                nc.vector.tensor_copy(out=o, in_=i)
+            else:
+                nc.scalar.copy(out=o, in_=i)
 
         def quant(w, g, t0, t1):
             c = slice(t0 * P, t1 * P)
@@ -128,48 +120,62 @@ def tile_barotropicvorticitytransformtendency_x1_kernel(
                 start=start, stop=stop,
             )
 
-        def unit(g, b0, n, ts):
-            k = len(ts)
+        s_of, v_of = {}, {}
+
+        def parts(pool, name, order, ts, n):
+            if n == B:
+                out = []
+                for i in (0, 1):
+                    bank = pool.tile([P, 1, 1, B], F32, name=name)
+                    out.append((bank, [(0, i, bank[:, 0, 0, :])]))
+                return out
+            bank = pool.tile([P, len(ts), 2, n], F32, name=name)
+            return [(bank, [(j, i, bank[:, j, i, :]) for j in range(len(ts)) for i in (0, 1)])]
+
+        def mm_s(g, b0, n, ts):
             b = slice(b0, b0 + n)
-            sb, vb = [], []
-            parts = []
-            if n == B:
-                for i in (0, 1):
-                    sb.append(ps_s.tile([P, B], F32, name="s_bank"))
-                parts_s = [(ts[0], i, sb[i][:]) for i in (0, 1)]
-            else:
-                bank = ps_s.tile([P, k, 2, n], F32, name="s_bank")
-                parts_s = [(t, i, bank[:, j, i, :]) for j, t in enumerate(ts) for i in (0, 1)]
-            for t, i, o in parts_s:
-                w = ("dx", "dy")[i]
-                c = slice(t * P, (t + 1) * P)
-                mm(o, cod[w, g][:, c], sca[w, g][:, c], zc_q[:, b], zc_s[:, b])
-            if n == B:
-                for i in (0, 1):
-                    vb.append(ps_v.tile([P, B], F32, name="v_bank"))
-                parts_v = [(ts[0], i, vb[i][:]) for i in (0, 1)]
-            else:
-                vbank = ps_v.tile([P, k, 2, n], F32, name="v_bank")
-                parts_v = [(t, i, vbank[:, j, i, :]) for j, t in enumerate(ts) for i in (0, 1)]
-            for t, i, o in parts_v:
-                w = ("dy", "dx")[i]
-                c = slice(t * P, (t + 1) * P)
-                mm(o, cod[w, g][:, c], sca[w, g][:, c], psi_q[:, b], psi_s[:, b])
-            s = stage.tile([P, k, 2, n], F32, name="s_sb")
-            for t, i, o in parts_s:
-                j = ts.index(t)
-                if i == 0:
-                    nc.scalar.activation(out=s[:, j, 0, :], in_=o, func=COPY, scale=wq_f[:, g, t : t + 1])
-                else:
-                    nc.scalar.activation(
-                        out=s[:, j, 1, :], in_=o, func=IDENTITY, scale=wq_f[:, g, t : t + 1], bias=bw_f[:, g, t : t + 1]
-                    )
+            s_of[g, b0, ts[0]] = parts(ps_s, "s_bank", ("dx", "dy"), ts, n)
+            for bank, ps in s_of[g, b0, ts[0]]:
+                for j, i, o in ps:
+                    w = ("dx", "dy")[i]
+                    c = slice(ts[j] * P, (ts[j] + 1) * P)
+                    mm(o, cod[w, g][:, c], sca[w, g][:, c], zc_q[:, b], zc_s[:, b])
+
+        def mm_v(g, b0, n, ts):
+            b = slice(b0, b0 + n)
+            v_of[g, b0, ts[0]] = parts(ps_v, "v_bank", ("dy", "dx"), ts, n)
+            for bank, ps in v_of[g, b0, ts[0]]:
+                for j, i, o in ps:
+                    w = ("dy", "dx")[i]
+                    c = slice(ts[j] * P, (ts[j] + 1) * P)
+                    mm(o, cod[w, g][:, c], sca[w, g][:, c], psi_q[:, b], psi_s[:, b])
+
+        s_sb = {}
+
+        def scale(g, b0, n, ts):
+            s = stage.tile([P, len(ts), 2, n], F32, name="s_sb")
+            s_sb[g, b0, ts[0]] = s
+            for bank, ps in s_of[g, b0, ts[0]]:
+                for j, i, o in ps:
+                    t = ts[j]
+                    if i == 0:
+                        nc.scalar.activation(out=s[:, j, 0, :], in_=o, func=COPY, scale=wq_f[:, g, t : t + 1])
+                    else:
+                        nc.scalar.activation(
+                            out=s[:, j, 1, :], in_=o, func=IDENTITY, scale=wq_f[:, g, t : t + 1], bias=bw_f[:, g, t : t + 1]
+                        )
+
+        def times(g, b0, n, ts):
+            s = s_sb[g, b0, ts[0]]
             m = m_sb[g]
+            vb = v_of[g, b0, ts[0]]
             if n == B:
                 for i in (0, 1):
-                    nc.vector.tensor_tensor(out=m[:, ts[0], i, :], in0=vb[i][:], in1=s[:, 0, i, :], op=MULT)
+                    nc.vector.tensor_tensor(out=m[:, ts[0], i, :], in0=vb[i][0][:, 0, 0, :], in1=s[:, 0, i, :], op=MULT)
             else:
-                nc.vector.tensor_tensor(out=m[:, ts[0] : ts[0] + k, :, b], in0=vbank[:], in1=s[:], op=MULT)
+                nc.vector.tensor_tensor(
+                    out=m[:, ts[0] : ts[0] + len(ts), :, b0 : b0 + n], in0=vb[0][0][:], in1=s[:], op=MULT
+                )
 
         def subtract(eng, g, b0, n):
             b = slice(b0, b0 + n)
@@ -245,67 +251,117 @@ def tile_barotropicvorticitytransformtendency_x1_kernel(
         def quant_all(q, s, g):
             nc.vector.quantize_mx(out=q[:].bitcast(FP8X4), scales=s[:], in_=g[:].rearrange("p b t -> p (b t)"))
 
-        nc.scalar.activation(out=wq_f[:], in_=wq_b[:], func=COPY)
+        load("dx", dx[:, 0:512], 0)
+        nc.sync.dma_start(out=psi_sb[:, 0:2, :], in_=psi_v[:, 0:2, :])
+        nc.sync.dma_start(out=psi_sb[:, 2:4, :], in_=psi_v[:, 2:4, :])
+        nc.sync.dma_start(out=kap[:], in_=kappa.rearrange("(p t) -> p t", t=4))
+        load("dy", dy[:, 0:512], 0)
+        nc.sync.dma_start(out=wq_b[:], in_=wq.rearrange("(g p t) -> p g t", g=2, t=4))
+        nc.sync.dma_start(out=beta_b[:], in_=beta.rearrange("(g p t) -> p g t", g=2, t=4))
+        load("p", p[0:512, :], 0)
+        load("dx", dx[:, 512:1024], 1)
+        load("dy", dy[:, 512:1024], 1)
+        load("p", p[512:1024, :], 1)
+        nc.gpsimd.tensor_copy(out=wq_f[:], in_=wq_b[:])
         nc.gpsimd.tensor_tensor(out=bw_f[:], in0=beta_b[:], in1=wq_b[:], op=MULT)
-        inter("dx", 0, 64)
+        inter("v", "dx", 0, 0, 88)
+        inter("s", "dx", 0, 88, 128)
         xt0 = turn(0)
         xt1 = turn(1)
-        quant("dx", 0, 0, 4)
         turn_out("s", 0, xt0)
-        turn_out("v", 1, xt1)
-        inter("dy", 0, 72)
-        quant_all(psi_q, psi_s, psi_g)
+        turn_out("s", 1, xt1)
+        quant("dx", 0, 0, 4)
+        inter("v", "dy", 0, 0, 80)
+        inter("s", "dy", 0, 80, 128)
         nc.vector.tensor_tensor(out=zc_g[:], in0=psi_g[:], in1=kap[:].unsqueeze(1).to_broadcast([P, B, 4]), op=MULT)
         quant("dy", 0, 0, 4)
-        inter("dx", 1, 48)
         quant_all(zc_q, zc_s, zc_g)
-        inter("dy", 1, 80)
-        quant("dx", 1, 0, 4)
-        inter("p", 0, 64)
-        unit(0, 0, B, [0])
-        unit(0, 0, B, [1])
-        quant("dy", 1, 0, 4)
-        unit(0, 0, B, [2])
-        unit(0, 0, B, [3])
-        for i in range(8):
-            subtract(nc.gpsimd, 0, 64 * i, 64)
+        inter("s", "p", 0, 0, 128)
+        inter("v", "dx", 1, 0, 128)
+        mm_s(0, 0, B, [0])
+        scale(0, 0, B, [0])
+        quant_all(psi_q, psi_s, psi_g)
         quant("p", 0, 0, 4)
-        inter("p", 1, 40)
-        unit(1, 0, 256, [0])
-        unit(1, 0, 256, [1])
-        unit(1, 0, 256, [2])
-        unit(1, 0, 256, [3])
+        mm_s(0, 0, B, [1])
+        scale(0, 0, B, [1])
+        inter("v", "dy", 1, 0, 40)
+        mm_v(0, 0, B, [0])
+        times(0, 0, B, [0])
+        mm_s(0, 0, B, [2])
+        scale(0, 0, B, [2])
+        mm_v(0, 0, B, [1])
+        times(0, 0, B, [1])
+        mm_s(0, 0, B, [3])
+        scale(0, 0, B, [3])
+        mm_v(0, 0, B, [2])
+        quant("dx", 1, 0, 4)
+        inter("s", "dy", 1, 40, 128)
+        times(0, 0, B, [2])
+        inter("s", "p", 1, 0, 128)
+        mm_v(0, 0, B, [3])
+        times(0, 0, B, [3])
+        quant("dy", 1, 0, 4)
+        mm_s(1, 0, 256, [0])
+        scale(1, 0, 256, [0])
+        mm_v(1, 0, 256, [0])
+        mm_s(1, 0, 256, [1])
+        scale(1, 0, 256, [1])
+        mm_v(1, 0, 256, [1])
+        subtract(nc.vector, 0, 0, 256)
+        mm_s(1, 0, 256, [2])
+        scale(1, 0, 256, [2])
+        mm_v(1, 0, 256, [2])
+        subtract(nc.vector, 0, 256, 256)
+        mm_s(1, 0, 256, [3])
+        scale(1, 0, 256, [3])
         quant("p", 1, 0, 4)
-        unit(1, 256, 128, [0, 1])
-        subtract(nc.vector, 1, 0, 256)
-        unit(1, 256, 128, [2, 3])
+        times(1, 0, 256, [0])
+        mm_v(1, 0, 256, [3])
+        mm_s(1, 256, 128, [0, 1])
+        scale(1, 256, 128, [0, 1])
+        times(1, 0, 256, [1])
+        mm_v(1, 256, 128, [0, 1])
+        times(1, 0, 256, [2])
+        mm_s(1, 256, 128, [2, 3])
+        scale(1, 256, 128, [2, 3])
+        times(1, 0, 256, [3])
         quant_jw(0, 0, 512)
+        mm_v(1, 256, 128, [2, 3])
+        subtract(nc.vector, 1, 0, 256)
+        mm_s(1, 384, 128, [0, 1])
+        scale(1, 384, 128, [0, 1])
+        mm_s(1, 384, 128, [2, 3])
+        scale(1, 384, 128, [2, 3])
+        times(1, 256, 128, [0, 1])
         quant_jw(1, 0, 256)
-        unit(1, 384, 128, [0, 1])
-        subtract(nc.vector, 1, 256, 128)
-        unit(1, 384, 128, [2, 3])
-        k0 = planes_mm(0)
-        planes_out("s", 0, k0)
+        mm_v(1, 384, 128, [0, 1])
+        times(1, 256, 128, [2, 3])
         r0 = rows_mm(0, "s")
         rows_out("s", 0, r0)
-        quant_jw(1, 256, 128)
+        times(1, 384, 128, [0, 1])
+        k0 = planes_mm(0)
+        planes_out("s", 0, k0)
+        subtract(nc.vector, 1, 256, 128)
+        mm_v(1, 384, 128, [2, 3])
+        times(1, 384, 128, [2, 3])
         k1 = planes_mm(1)
+        quant_jw(1, 256, 128)
         planes_out("s", 1, k1)
         r1 = rows_mm(1, "s")
         rows_out("s", 1, r1)
-        subtract(nc.vector, 1, 384, 128)
-        k2 = planes_mm(2)
-        planes_out("s", 2, k2)
-        quant_jw(1, 384, 128)
         r2 = rows_mm(2, "v")
-        rows_out("s", 2, r2)
+        k2 = planes_mm(2)
+        subtract(nc.vector, 1, 384, 128)
         quant_y(0, 256)
         store_words(nc.sync, 0, 256)
+        quant_jw(1, 384, 128)
+        rows_out("s", 2, r2)
+        planes_out("v", 2, k2)
         k3 = planes_mm(3)
         r3 = rows_mm(3, "s")
         quant_y(256, 128)
-        planes_out("v", 3, k3)
-        rows_out("s", 3, r3)
+        planes_out("s", 3, k3)
         quant_y(384, 128)
         store_words(nc.sync, 256, 256)
+        rows_out("s", 3, r3)
         store_scales(nc.sync, 0, 512)

from contextlib import ExitStack

import concourse.mybir as mybir
from concourse.masks import make_identity

B, L, G = 512, 512, 1024
FLOPS = 5 * 2 * B * L * G

F32 = mybir.dt.float32
BF16 = mybir.dt.bfloat16
U32 = mybir.dt.uint32
I32 = mybir.dt.int32
U8 = mybir.dt.uint8
FP8X4 = mybir.dt.float8_e4m3fn_x4
ADD = mybir.AluOpType.add
SUB = mybir.AluOpType.subtract
MULT = mybir.AluOpType.mult
COPY = mybir.ActivationFunctionType.Copy
IDENTITY = mybir.ActivationFunctionType.Identity

P = 128
H = 256


def tile_barotropicvorticitytransformtendency_x1_kernel(
    tc, psi, kappa, dx, dy, beta, wq, p, out_0, out_1, out_2
):
    nc = tc.nc
    with ExitStack() as ctx:
        ctx.enter_context(tc.manual_schedule())
        keep = ctx.enter_context(tc.tile_pool(name="keep", bufs=1))
        stage = ctx.enter_context(tc.tile_pool(name="stage", bufs=4))
        prod = ctx.enter_context(tc.tile_pool(name="prod", bufs=3))
        ps_s = ctx.enter_context(tc.psum_pool(name="ps_s", bufs=3))
        ps_v = ctx.enter_context(tc.psum_pool(name="ps_v", bufs=3))
        ps_o = ctx.enter_context(tc.psum_pool(name="ps_o", bufs=2))

        ident = keep.tile([P, P], F32, name="ident")
        kap = keep.tile([P, 4], BF16, name="kap")
        wq_b = keep.tile([P, 2, 4], BF16, name="wq_b")
        wq_f = keep.tile([P, 2, 4], F32, name="wq_f")
        beta_b = keep.tile([P, 2, 4], BF16, name="beta_b")
        bw_f = keep.tile([P, 2, 4], F32, name="bw_f")
        psi_sb = keep.tile([P, 4, L], BF16, name="psi_sb", align_bytes=64)
        psi_g = keep.tile([P, B, 4], BF16, name="psi_g", align_bytes=64)
        zc_g = keep.tile([P, B, 4], BF16, name="zc_g", align_bytes=64)
        psi_q = keep.tile([P, B], U32, name="psi_q", align_bytes=64)
        psi_s = keep.tile([P, B], U8, name="psi_s", align_bytes=64)
        zc_q = keep.tile([P, B], U32, name="zc_q", align_bytes=64)
        zc_s = keep.tile([P, B], U8, name="zc_s", align_bytes=64)

        raw, grp, cod, sca = {}, {}, {}, {}
        for w in ("dx", "dy", "p"):
            for g in (0, 1):
                raw[w, g] = keep.tile([P, 4, 512], BF16, name="raw_%s%d" % (w, g), align_bytes=64)
                grp[w, g] = keep.tile([P, 4, P, 4], BF16, name="grp_%s%d" % (w, g), align_bytes=64)
                cod[w, g] = keep.tile([P, 512], U32, name="cod_%s%d" % (w, g), align_bytes=64)
                sca[w, g] = keep.tile([P, 512], U8, name="sca_%s%d" % (w, g), align_bytes=64)
        jw_g, jw_q, jw_s = {}, {}, {}
        for g in (0, 1):
            jw_g[g] = keep.tile([P, B, 4], BF16, name="jw_g%d" % g, align_bytes=64)
            jw_q[g] = keep.tile([P, B], U32, name="jw_q%d" % g, align_bytes=64)
            jw_s[g] = keep.tile([P, B], U8, name="jw_s%d" % g, align_bytes=64)
        m_sb = {}
        for g in (0, 1):
            m_sb[g] = keep.tile([P, 4, 2, B], F32, name="m_sb%d" % g)
        y_g = keep.tile([P, B, 4], BF16, name="y_g", align_bytes=64)
        y_q = keep.tile([P, B], U32, name="y_q", align_bytes=64)
        y_s = keep.tile([P, B], U8, name="y_s", align_bytes=64)

        def load(w, ap, g):
            nc.sync.dma_start(out=raw[w, g][:], in_=ap.rearrange("(p j) m -> p j m", j=4))

        psi_v = psi.rearrange("(p c) l -> p c l", c=4)

        make_identity(nc, ident[:])

        def inter(eng, w, g, m0, m1):
            if m0 == m1:
                return
            o = grp[w, g][:].rearrange("p t m j -> p m t j")[:, m0:m1]
            i = raw[w, g][:].rearrange("p j (m t) -> p m t j", t=4)[:, m0:m1]
            if eng == "v":
                nc.vector.tensor_copy(out=o, in_=i)
            else:
                nc.scalar.copy(out=o, in_=i)

        def quant(w, g, t0, t1):
            c = slice(t0 * P, t1 * P)
            nc.vector.quantize_mx(
                out=cod[w, g][:, c].bitcast(FP8X4),
                scales=sca[w, g][:, c],
                in_=grp[w, g][:, t0:t1, :, :].rearrange("p t m j -> p (t m j)"),
            )

        words = psi_sb[:].rearrange("p c l -> p (c l)").bitcast(F32)

        def turn(k):
            xt = ps_o.tile([P, 512], F32, name="o_bank")
            for c in (0, 1):
                for u in (0, 1):
                    w0 = 256 * (2 * k + c)
                    s0 = P * (2 * c + u)
                    nc.tensor.transpose(xt[:, s0 : s0 + P], words[:, w0 + u : w0 + 256 : 2], ident[:])
            return xt

        psi_w = psi_g[:].rearrange("p b t -> p (b t)").bitcast(F32).rearrange("p (r k c u) -> p r k c u", k=2, c=2, u=2)

        def turn_out(eng, k, xt):
            o = psi_w[:, :, k, :, :]
            i = xt[:].rearrange("p (c u r) -> p r c u", c=2, u=2)
            if eng == "v":
                nc.vector.tensor_copy(out=o, in_=i)
            else:
                nc.scalar.copy(out=o, in_=i)

        def mm(out, a, asc, b, bsc, start=True, stop=True):
            nc.tensor.matmul_mx(
                out=out, lhsT=a.bitcast(FP8X4), lhsT_scale=asc, rhs=b.bitcast(FP8X4), rhs_scale=bsc,
                start=start, stop=stop,
            )

        s_of, v_of = {}, {}

        def parts(pool, name, order, ts, n):
            if n == B:
                out = []
                for i in (0, 1):
                    bank = pool.tile([P, 1, 1, B], F32, name=name)
                    out.append((bank, [(0, i, bank[:, 0, 0, :])]))
                return out
            bank = pool.tile([P, len(ts), 2, n], F32, name=name)
            return [(bank, [(j, i, bank[:, j, i, :]) for j in range(len(ts)) for i in (0, 1)])]

        def mm_s(g, b0, n, ts):
            b = slice(b0, b0 + n)
            s_of[g, b0, ts[0]] = parts(ps_s, "s_bank", ("dx", "dy"), ts, n)
            for bank, ps in s_of[g, b0, ts[0]]:
                for j, i, o in ps:
                    w = ("dx", "dy")[i]
                    c = slice(ts[j] * P, (ts[j] + 1) * P)
                    mm(o, cod[w, g][:, c], sca[w, g][:, c], zc_q[:, b], zc_s[:, b])

        def mm_v(g, b0, n, ts):
            b = slice(b0, b0 + n)
            v_of[g, b0, ts[0]] = parts(ps_v, "v_bank", ("dy", "dx"), ts, n)
            for bank, ps in v_of[g, b0, ts[0]]:
                for j, i, o in ps:
                    w = ("dy", "dx")[i]
                    c = slice(ts[j] * P, (ts[j] + 1) * P)
                    mm(o, cod[w, g][:, c], sca[w, g][:, c], psi_q[:, b], psi_s[:, b])

        s_sb = {}

        def scale(g, b0, n, ts):
            s = stage.tile([P, len(ts), 2, n], F32, name="s_sb")
            s_sb[g, b0, ts[0]] = s
            for bank, ps in s_of[g, b0, ts[0]]:
                for j, i, o in ps:
                    t = ts[j]
                    if i == 0:
                        nc.scalar.activation(out=s[:, j, 0, :], in_=o, func=COPY, scale=wq_f[:, g, t : t + 1])
                    else:
                        nc.scalar.activation(
                            out=s[:, j, 1, :], in_=o, func=IDENTITY, scale=wq_f[:, g, t : t + 1], bias=bw_f[:, g, t : t + 1]
                        )

        def times(g, b0, n, ts):
            s = s_sb[g, b0, ts[0]]
            m = m_sb[g]
            vb = v_of[g, b0, ts[0]]
            if n == B:
                for i in (0, 1):
                    nc.vector.tensor_tensor(out=m[:, ts[0], i, :], in0=vb[i][0][:, 0, 0, :], in1=s[:, 0, i, :], op=MULT)
            else:
                nc.vector.tensor_tensor(
                    out=m[:, ts[0] : ts[0] + len(ts), :, b0 : b0 + n], in0=vb[0][0][:], in1=s[:], op=MULT
                )

        def subtract(eng, g, b0, n):
            b = slice(b0, b0 + n)
            eng.tensor_tensor(
                out=jw_g[g][:, b, :].rearrange("p (c i) t -> p c t i", i=4),
                in0=m_sb[g][:, :, 1, b].rearrange("p t (c i) -> p c t i", i=4),
                in1=m_sb[g][:, :, 0, b].rearrange("p t (c i) -> p c t i", i=4),
                op=SUB,
            )

        def quant_jw(g, b0, n):
            b = slice(b0, b0 + n)
            nc.vector.quantize_mx(
                out=jw_q[g][:, b].bitcast(FP8X4),
                scales=jw_s[g][:, b],
                in_=jw_g[g][:, b, :].rearrange("p b t -> p (b t)"),
            )

        def planes_mm(c):
            bank = ps_o.tile([P, 512], F32, name="o_bank")
            b = slice(c * P, (c + 1) * P)
            for t in range(4):
                l = slice(t * P, (t + 1) * P)
                for g in (0, 1):
                    mm(bank[:, l], cod["p", g][:, l], sca["p", g][:, l], jw_q[g][:, b], jw_s[g][:, b],
                       start=g == 0, stop=g == 1)
            return bank

        def rows_mm(c, pool, gs=(0, 1), bank=None):
            if bank is None:
                if pool == "s":
                    bank = ps_s.tile([P, B], F32, name="s_bank")
                elif pool == "v":
                    bank = ps_v.tile([P, B], F32, name="v_bank")
                else:
                    bank = ps_o.tile([P, B], F32, name="o_bank")
            b = slice(c * P, (c + 1) * P)
            for g in gs:
                mm(bank[:], jw_q[g][:, b], jw_s[g][:, b], cod["p", g][:], sca["p", g][:], start=g == 0, stop=g == 1)
            return bank

        def negate(eng, out, in_):
            if eng == "v":
                nc.vector.tensor_scalar(out=out, in0=in_, scalar1=-1.0, scalar2=None, op0=MULT)
            else:
                nc.scalar.activation(out=out, in_=in_, func=COPY, scale=-1.0)

        def planes_out(eng, c, bank):
            negate(eng, y_g[:, c * P : (c + 1) * P, :], bank[:].rearrange("p (t b) -> p b t", t=4))

        def rows_out(eng, c, bank):
            rows = stage.tile([P, 512], F32, name="rows")
            negate(eng, rows[:].rearrange("p (m t) -> p m t", t=4), bank[:].rearrange("p (t m) -> p m t", t=4))
            nc.sync.dma_start(out=out_0[c * P : (c + 1) * P, :], in_=rows[:])

        def quant_y(b0, n):
            b = slice(b0, b0 + n)
            nc.vector.quantize_mx(
                out=y_q[:, b].bitcast(FP8X4), scales=y_s[:, b], in_=y_g[:, b, :].rearrange("p b t -> p (b t)")
            )

        def store_words(q, b0, n):
            b = slice(b0, b0 + n)
            q.dma_start(out=out_1[0, :, b, :].rearrange("p b t -> p (b t)").bitcast(I32), in_=y_q[:, b].bitcast(I32))

        def store_scales(q, b0, n):
            b = slice(b0, b0 + n)
            for i in range(4):
                q.dma_start(
                    out=out_2[0, 4 * i : 4 * i + 4, b].bitcast(I32), in_=y_s[32 * i : 32 * i + 4, b].bitcast(I32)
                )

        def quant_all(q, s, g):
            nc.vector.quantize_mx(out=q[:].bitcast(FP8X4), scales=s[:], in_=g[:].rearrange("p b t -> p (b t)"))

        load("dx", dx[:, 0:512], 0)
        nc.sync.dma_start(out=psi_sb[:, 0:2, :], in_=psi_v[:, 0:2, :])
        nc.sync.dma_start(out=psi_sb[:, 2:4, :], in_=psi_v[:, 2:4, :])
        nc.sync.dma_start(out=kap[:], in_=kappa.rearrange("(p t) -> p t", t=4))
        load("dy", dy[:, 0:512], 0)
        nc.sync.dma_start(out=wq_b[:], in_=wq.rearrange("(g p t) -> p g t", g=2, t=4))
        nc.sync.dma_start(out=beta_b[:], in_=beta.rearrange("(g p t) -> p g t", g=2, t=4))
        load("p", p[0:512, :], 0)
        load("dx", dx[:, 512:1024], 1)
        load("dy", dy[:, 512:1024], 1)
        load("p", p[512:1024, :], 1)
        nc.gpsimd.tensor_copy(out=wq_f[:], in_=wq_b[:])
        nc.gpsimd.tensor_tensor(out=bw_f[:], in0=beta_b[:], in1=wq_b[:], op=MULT)
        inter("v", "dx", 0, 0, 88)
        inter("s", "dx", 0, 88, 128)
        xt0 = turn(0)
        xt1 = turn(1)
        turn_out("s", 0, xt0)
        turn_out("s", 1, xt1)
        quant("dx", 0, 0, 4)
        inter("v", "dy", 0, 0, 80)
        inter("s", "dy", 0, 80, 128)
        nc.vector.tensor_tensor(out=zc_g[:], in0=psi_g[:], in1=kap[:].unsqueeze(1).to_broadcast([P, B, 4]), op=MULT)
        quant("dy", 0, 0, 4)
        quant_all(zc_q, zc_s, zc_g)
        inter("s", "p", 0, 0, 128)
        inter("v", "dx", 1, 0, 128)
        mm_s(0, 0, B, [0])
        scale(0, 0, B, [0])
        quant_all(psi_q, psi_s, psi_g)
        quant("p", 0, 0, 4)
        mm_s(0, 0, B, [1])
        scale(0, 0, B, [1])
        inter("v", "dy", 1, 0, 40)
        mm_v(0, 0, B, [0])
        times(0, 0, B, [0])
        mm_s(0, 0, B, [2])
        scale(0, 0, B, [2])
        mm_v(0, 0, B, [1])
        times(0, 0, B, [1])
        mm_s(0, 0, B, [3])
        scale(0, 0, B, [3])
        mm_v(0, 0, B, [2])
        quant("dx", 1, 0, 4)
        inter("s", "dy", 1, 40, 128)
        times(0, 0, B, [2])
        inter("s", "p", 1, 0, 128)
        mm_v(0, 0, B, [3])
        times(0, 0, B, [3])
        quant("dy", 1, 0, 4)
        mm_s(1, 0, 256, [0])
        scale(1, 0, 256, [0])
        mm_v(1, 0, 256, [0])
        mm_s(1, 0, 256, [1])
        scale(1, 0, 256, [1])
        mm_v(1, 0, 256, [1])
        subtract(nc.vector, 0, 0, 256)
        mm_s(1, 0, 256, [2])
        scale(1, 0, 256, [2])
        mm_v(1, 0, 256, [2])
        subtract(nc.vector, 0, 256, 256)
        mm_s(1, 0, 256, [3])
        scale(1, 0, 256, [3])
        quant("p", 1, 0, 4)
        times(1, 0, 256, [0])
        mm_v(1, 0, 256, [3])
        mm_s(1, 256, 128, [0, 1])
        scale(1, 256, 128, [0, 1])
        times(1, 0, 256, [1])
        mm_v(1, 256, 128, [0, 1])
        times(1, 0, 256, [2])
        mm_s(1, 256, 128, [2, 3])
        scale(1, 256, 128, [2, 3])
        times(1, 0, 256, [3])
        quant_jw(0, 0, 512)
        mm_v(1, 256, 128, [2, 3])
        subtract(nc.vector, 1, 0, 256)
        mm_s(1, 384, 128, [0, 1])
        scale(1, 384, 128, [0, 1])
        mm_s(1, 384, 128, [2, 3])
        scale(1, 384, 128, [2, 3])
        times(1, 256, 128, [0, 1])
        quant_jw(1, 0, 256)
        mm_v(1, 384, 128, [0, 1])
        times(1, 256, 128, [2, 3])
        r0 = rows_mm(0, "s")
        rows_out("s", 0, r0)
        times(1, 384, 128, [0, 1])
        k0 = planes_mm(0)
        planes_out("s", 0, k0)
        subtract(nc.vector, 1, 256, 128)
        mm_v(1, 384, 128, [2, 3])
        times(1, 384, 128, [2, 3])
        k1 = planes_mm(1)
        quant_jw(1, 256, 128)
        planes_out("s", 1, k1)
        r1 = rows_mm(1, "s")
        rows_out("s", 1, r1)
        r2 = rows_mm(2, "v")
        k2 = planes_mm(2)
        subtract(nc.vector, 1, 384, 128)
        quant_y(0, 256)
        store_words(nc.sync, 0, 256)
        quant_jw(1, 384, 128)
        rows_out("s", 2, r2)
        planes_out("v", 2, k2)
        k3 = planes_mm(3)
        r3 = rows_mm(3, "s")
        quant_y(256, 128)
        planes_out("s", 3, k3)
        quant_y(384, 128)
        store_words(nc.sync, 256, 256)
        rows_out("s", 3, r3)
        store_scales(nc.sync, 0, 512)
